import numpy as np
import ml_dtypes


def mxq(x, axis, fmt="e4m3"):
    dtype, down = {"e4m3": (ml_dtypes.float8_e4m3fn, 7), "e5m2": (ml_dtypes.float8_e5m2, 14)}[fmt]
    v = np.moveaxis(np.asarray(x, np.float32).astype(ml_dtypes.bfloat16).astype(np.float64), axis, -1)
    blocks = v.reshape(v.shape[:-1] + (-1, 32))
    amax = np.abs(blocks).max(-1, keepdims=True)
    byte = np.maximum(np.where(amax > 0, np.frexp(amax)[1] - 1 + 127, 0) - down, 1)
    scale = np.exp2(byte - 127.0)
    codes = (blocks / scale).astype(np.float32).astype(dtype).astype(np.float64)
    return np.moveaxis((codes * scale).reshape(v.shape), -1, axis)


WIDE = False


def mx_kscale(k):
    if not WIDE:
        return np.ones(k)
    levels = np.array([10, -10, 5, -5, 0])
    if k % 512:
        return np.exp2(np.random.permutation(np.resize(levels, k // 32))).repeat(32)
    a = np.empty((k // 512, 16))
    for p in range(k // 512):
        a[p, :8] = np.random.permutation(np.resize(levels, 8))
        for g in range(8):
            far = levels[np.abs(levels - a[p, g]) >= 10]
            a[p, g + 8] = far[np.random.randint(len(far))]
    return np.exp2(a.ravel()).repeat(32)


def f64(x):
    return np.asarray(x).astype(np.float64)


def striped(idx):
    return np.tile(idx.reshape(-1, 16).T, (8, 1)).astype(np.uint16)


def unstriped(offs):
    return offs[:16].T.reshape(-1).astype(np.int64)


def striped8(idx):
    return np.concatenate([x.reshape(-1, 16).T for x in idx]).astype(np.uint16)


def runs(offs, k):
    lists = np.stack([offs[16 * r : 16 * r + 16].T.reshape(-1) for r in range(8)]).astype(np.int64)
    return lists[np.arange(k) % 512 // 64]


def pack_weight(w):
    k, n = w.shape
    w = f64(np.asarray(w, np.float32).astype(ml_dtypes.bfloat16)).reshape(k // 32, 32, n)
    amax = np.abs(w).max(1)
    byte = np.clip(np.where(amax > 0, np.frexp(amax)[1] - 1 + 127 - 7, 1), 1, 254)
    scaled = (w * np.exp2(127.0 - byte)[:, None, :]).reshape(k, n).astype(np.float32)
    words = np.ascontiguousarray(scaled.reshape(k // 512, 128, 4, n).transpose(0, 1, 3, 2)).astype(ml_dtypes.float8_e4m3fn).view(np.uint8)
    return words, np.ascontiguousarray(byte.astype(np.uint8).reshape(k // 512, 16, n))


def unpack_weight(words, scales):
    g, p, n, _ = words.shape
    vals = np.ascontiguousarray(words).view(ml_dtypes.float8_e4m3fn).astype(np.float64) * np.repeat(np.exp2(scales.astype(np.float64) - 127.0), 8, axis=1)[..., None]
    return vals.transpose(0, 1, 3, 2).reshape(g * 512, n)


K, T, S, G, H, W, U = 512, 2048, 512, 2048, 512, 256, 1024


def setup_inputs():
    n = np.random.standard_normal
    s = mx_kscale(K)[:, None]
    packed_xT = pack_weight(n((K, T)) * s)
    packed_dT = pack_weight(n((K, G)) / s)
    perm = np.stack([np.random.permutation(S) for _ in range(8)])
    return {
        "x_words": packed_xT[0],
        "x_scales": packed_xT[1],
        "d_words": packed_dT[0],
        "d_scales": packed_dT[1],
        "gs": (np.random.uniform(0.5, 1.5, (K, 1)) * s).astype(np.float32),
        "mem": n((H, U)).astype(np.float32),
        "offs": striped(np.random.permutation(T)[:S]),
        "ci": striped(np.random.permutation(G)[:H]),
        "n1": striped8(perm[:, :W]),
        "n2": striped8(perm[:, W:]),
        "n3": striped8(np.stack([np.random.permutation(S) for _ in range(8)])),
        "k1": striped8(np.random.randint(0, G, (8, H))),
        "n4": striped8(np.stack([np.random.permutation(U)[:S] for _ in range(8)])),
    }


def reference(x_words, x_scales, d_words, d_scales, gs, mem, offs, ci, n1, n2, n3, k1, n4):
    d_k1 = unpack_weight(d_words, d_scales)[np.arange(K)[:, None], runs(k1, K)]
    d_ci = unpack_weight(d_words, d_scales)[:, unstriped(ci)]
    xq = unpack_weight(x_words, x_scales)[:, unstriped(offs)]
    s = 0.0625 * (d_ci.T @ xq)
    pa = s[np.arange(H)[:, None], runs(n1, H)]
    pb = s[np.arange(H)[:, None], runs(n2, H)]
    rb = pa - pb
    ra = pa + pb
    ds = np.zeros((H, S))
    ds[np.arange(H)[:, None], runs(n1, H)] = ra
    dt = ds.copy()
    dt[np.arange(H)[:, None], runs(n2, H)] = rb
    z = f64(gs) * (np.maximum(dt, dt[np.arange(H)[:, None], runs(n3, H)]))
    h = 0.0625 * ((d_k1.T @ mxq(z, 0, "e4m3")))
    nw = np.maximum(h, 0.5 * (f64(mem)[np.arange(H)[:, None], runs(n4, H)]))
    out = f64(mem).copy()
    out[np.arange(H)[:, None], runs(n4, H)] = nw
    return out

@@ -1,0 +1,234 @@
+from contextlib import ExitStack
+
+import concourse.mybir as mybir
+
+K, T, S, G, H, W, U = 512, 2048, 512, 2048, 512, 256, 1024
+FLOPS = 2 * K * H * S + 2 * H * H * S
+
+F32 = mybir.dt.float32
+BF16 = mybir.dt.bfloat16
+I32 = mybir.dt.int32
+U32 = mybir.dt.uint32
+U16 = mybir.dt.uint16
+U8 = mybir.dt.uint8
+FP8X4 = mybir.dt.float8_e4m3fn_x4
+ALU = mybir.AluOpType
+COPY = mybir.ActivationFunctionType.Copy
+
+P = 128
+PACK = 4
+HALF = S // 2
+PER_COL = 16
+
+
+def tile_picked_dwqhaarhpagex_none_p_kernel(
+    tc, x_words, x_scales, d_words, d_scales, gs, mem, offs, ci, n1, n2, n3, k1, n4, out
+):
+    nc = tc.nc
+    with ExitStack() as ctx:
+        lists = ctx.enter_context(tc.tile_pool(name="lists", bufs=1))
+        held = ctx.enter_context(tc.tile_pool(name="held", bufs=1))
+        psum = ctx.enter_context(tc.psum_pool(name="psum", bufs=8))
+
+        def load_list(name, src):
+            tile = lists.tile([P, src.shape[1]], U16, name=name)
+            nc.sync.dma_start(tile[:], src)
+            return tile
+
+        def load_words(name, src):
+            tile = held.tile([P, src.shape[2]], U32, name=name, tag=name, align_bytes=64)
+            nc.sync.dma_start(tile[:].bitcast(I32), src[0].rearrange("p n t -> p (n t)").bitcast(I32))
+            return tile
+
+        def load_plane(name, src, clear):
+            tile = held.tile([P, src.shape[2]], U8, name=name, tag=name, align_bytes=64)
+            clear.memset(tile[:].bitcast(I32), 0)
+            for q in range(4):
+                nc.scalar.dma_start(tile[32 * q : 32 * q + 4, :].bitcast(I32), src[0, 4 * q : 4 * q + 4, :].bitcast(I32))
+            return tile
+
+        d_plane = load_plane("d_plane", d_scales, nc.vector)
+        x_plane = load_plane("x_plane", x_scales, nc.gpsimd)
+        ci_l = load_list("ci_l", ci)
+        offs_l = load_list("offs_l", offs)
+        d_tab = load_words("d_tab", d_words)
+        x_tab = load_words("x_tab", x_words)
+        k1_l = load_list("k1_l", k1)
+        run_plane = held.tile([P, G], U8, name="run_plane", tag="run_plane", align_bytes=64)
+        nc.vector.memset(run_plane[:].bitcast(I32), 0)
+        for b in range(2):
+            nc.sync.dma_start(run_plane[b:P:16, :].bitcast(I32), d_scales[0, b:16:2, :].bitcast(I32))
+        n1_l = load_list("n1_l", n1)
+        n2_l = load_list("n2_l", n2)
+        n3_l = load_list("n3_l", n3)
+        n4_l = load_list("n4_l", n4)
+        gs_t = held.tile([P, PACK], F32, name="gs_t")
+        nc.sync.dma_start(gs_t[:], gs.rearrange("(p t) o -> p (t o)", t=PACK))
+        mem_rows = mem.rearrange("(p t) u -> t p u", t=PACK)
+        out_rows = out.rearrange("(p t) u -> t p u", t=PACK)
+
+        page = []
+        for t in range(PACK):
+            page.append(held.tile([P, U], F32, name="page%d" % t))
+            nc.sync.dma_start(page[t][:], mem_rows[t])
+
+        def dealt(tile):
+            return tile[:].rearrange("p (t m) -> p m t", t=PACK)
+
+        def in_order(tile):
+            return tile[:].rearrange("p (m t) -> p m t", t=PACK)
+
+        ci_scale = held.tile([P, H], U8, name="ci_scale", align_bytes=64)
+        nc.vector.tensor_copy(dealt(ci_scale), d_plane[:].indirect(ci_l[:]))
+        x_scale = held.tile([P, S], U8, name="x_scale", align_bytes=64)
+        nc.vector.tensor_copy(x_scale[:], x_plane[:].indirect(offs_l[:]))
+        ci_code = held.tile([P, H], U32, name="ci_code", tag="d_plane", align_bytes=64)
+        nc.vector.tensor_copy(dealt(ci_code), d_tab[:].indirect(ci_l[:]))
+        x_code = held.tile([P, S], U32, name="x_code", tag="x_plane", align_bytes=64)
+        nc.vector.tensor_copy(x_code[:], x_tab[:].indirect(offs_l[:]))
+
+        s_bank = []
+        for t in range(PACK):
+            cols = slice(t * P, (t + 1) * P)
+            s_bank.append(psum.tile([P, S], F32, name="bank"))
+            nc.tensor.matmul_mx(
+                out=s_bank[t][:], lhsT=ci_code[:, cols].bitcast(FP8X4), lhsT_scale=ci_scale[:, cols],
+                rhs=x_code[:].bitcast(FP8X4), rhs_scale=x_scale[:], start=True, stop=True,
+            )
+
+        k1_bytes = held.tile([P, H], U8, name="k1_bytes", tag="x_tab", align_bytes=64)
+        nc.vector.tensor_copy(k1_bytes[:], run_plane[:].indirect(k1_l[:]))
+        k1_bytes_dealt = held.tile([P, H], U8, name="k1_bytes_dealt")
+        nc.vector.tensor_copy(dealt(k1_bytes_dealt), in_order(k1_bytes))
+        k1_scale = held.tile([P, H], U8, name="k1_scale", align_bytes=64)
+        nc.gpsimd.memset(k1_scale[:].bitcast(I32), 0)
+        for odd in range(2):
+            for b in range(2):
+                nc.sync.dma_start(
+                    k1_scale[2 * odd + b : P : 32, :].bitcast(I32),
+                    k1_bytes_dealt[16 * odd + b : P : 32, :].bitcast(I32),
+                )
+
+        pa, pb, neg_pb, dt, far, top, half_old = {}, {}, {}, {}, {}, {}, {}
+        z_pairs = [held.tile([P, 2, HALF, 2], BF16, name="z_pairs%d" % c) for c in range(2)]
+        s = {}
+
+        def leave_bank(t):
+            s[t] = held.tile([P, S], F32, name="s%d" % t)
+            nc.scalar.activation(s[t][:], s_bank[t][:], COPY, scale=0.0625)
+
+        def fetch_pairs(t):
+            pa[t] = held.tile([P, W], F32, name="pa%d" % t)
+            neg_pb[t] = held.tile([P, W], F32, name="neg_pb%d" % t)
+            nc.scalar.activation(pa[t][:], s[t][:].indirect(n1_l[:]), COPY)
+            if t == 0:
+                nc.vector.tensor_scalar(neg_pb[t][:], s[t][:].indirect(n2_l[:]), -1.0, 0.0, ALU.mult, ALU.add)
+            else:
+                nc.scalar.activation(neg_pb[t][:], s[t][:].indirect(n2_l[:]), COPY, scale=-1.0)
+
+        def turn_sign(t):
+            pb[t] = held.tile([P, W], F32, name="pb%d" % t, tag="pb%d" % t, align_bytes=64)
+            nc.scalar.activation(pb[t][:], neg_pb[t][:], COPY, scale=-1.0)
+
+        def put_pairs(t):
+            dt[t] = held.tile([P, S], F32, name="dt", bufs=2)
+            nc.vector.tensor_tensor(dt[t][:].indirect(n2_l[:]), pa[t][:], neg_pb[t][:], ALU.add)
+            nc.vector.tensor_tensor(dt[t][:].indirect(n1_l[:]), pa[t][:], pb[t][:], ALU.add)
+
+        def cols_of(c):
+            return slice(c * HALF, (c + 1) * HALF)
+
+        def entries(lst, c):
+            return lst[:, c * HALF // PER_COL : (c + 1) * HALF // PER_COL]
+
+        def fetch_far(t):
+            far[t] = held.tile([P, S], F32, name="far%d" % t)
+            for c in range(2):
+                nc.scalar.activation(far[t][:, cols_of(c)], dt[t][:].indirect(entries(n3_l, c)), COPY)
+
+        def take_top(t, chunks):
+            top[t] = held.tile([P, S], F32, name="top%d" % t, tag="top%d" % t)
+            for cols in chunks:
+                nc.vector.tensor_tensor(top[t][:, cols], dt[t][:, cols], far[t][:, cols], ALU.max)
+
+        def weigh(t, c):
+            nc.scalar.activation(z_pairs[c][:, t // 2, :, t % 2], top[t][:, cols_of(c)], COPY, scale=gs_t[:, t : t + 1])
+
+        def fetch_old(t, slot):
+            half_old[t] = held.tile([P, S], F32, name="half_old%d" % t, tag=slot)
+            nc.scalar.activation(half_old[t][:], page[t][:].indirect(n4_l[:]), COPY, scale=0.5)
+
+        whole = [slice(0, S)]
+        leave_bank(0)
+        fetch_pairs(0)
+        leave_bank(1)
+        turn_sign(0)
+        fetch_pairs(1)
+        turn_sign(1)
+        put_pairs(0)
+        leave_bank(2)
+        fetch_pairs(2)
+        turn_sign(2)
+        put_pairs(1)
+        fetch_far(0)
+        leave_bank(3)
+        fetch_pairs(3)
+        turn_sign(3)
+        take_top(0, whole)
+        put_pairs(2)
+        fetch_far(1)
+        weigh(0, 0)
+        weigh(0, 1)
+        take_top(1, whole)
+        fetch_old(0, "top0")
+        put_pairs(3)
+        fetch_far(2)
+        weigh(1, 0)
+        weigh(1, 1)
+        fetch_old(1, "top1")
+        take_top(2, whole)
+        fetch_far(3)
+
+        k1_words = held.tile([P, H], U32, name="k1_words", tag="pb3", align_bytes=64)
+        nc.vector.tensor_copy(k1_words[:], d_tab[:].indirect(k1_l[:]))
+        k1_code = held.tile([P, H], U32, name="k1_code", align_bytes=64)
+        nc.vector.tensor_copy(dealt(k1_code), in_order(k1_words))
+
+        take_top(3, [cols_of(0), cols_of(1)])
+        z_code, z_scale = [], []
+        h_bank = {}
+        for c in range(2):
+            weigh(2, c)
+            weigh(3, c)
+            z = held.tile([P, HALF, 2], F32, name="z%d" % c, align_bytes=64)
+            nc.vector.tensor_copy(
+                z[:], z_pairs[c][:].rearrange("p u j e -> p u (j e)").bitcast(F32).rearrange("p u j -> p j u")
+            )
+            z_code.append(held.tile([P, HALF], U32, name="z_code%d" % c, align_bytes=64))
+            z_scale.append(held.tile([P, HALF], U8, name="z_scale%d" % c, align_bytes=64))
+            nc.vector.quantize_mx(
+                out=z_code[c][:].bitcast(FP8X4), scales=z_scale[c][:], in_=z[:].rearrange("p j u -> p (j u)").bitcast(BF16)
+            )
+            for t in range(PACK):
+                cols = slice(t * P, (t + 1) * P)
+                h_bank[t, c] = psum.tile([P, S], F32, name="bank")
+                nc.tensor.matmul_mx(
+                    out=h_bank[t, c][:, 0:HALF], lhsT=k1_code[:, cols].bitcast(FP8X4), lhsT_scale=k1_scale[:, cols],
+                    rhs=z_code[c][:].bitcast(FP8X4), rhs_scale=z_scale[c][:], start=True, stop=True,
+                )
+        fetch_old(2, "top2")
+        fetch_old(3, "top3")
+
+        def update(t, c):
+            new = held.tile([P, HALF], F32, name="new", bufs=2)
+            nc.vector.scalar_tensor_tensor(
+                new[:], h_bank[t, c][:, 0:HALF], 0.0625, half_old[t][:, cols_of(c)], ALU.mult, ALU.max
+            )
+            nc.vector.tensor_copy(page[t][:].indirect(entries(n4_l, c)), new[:])
+
+        for pair in ((0, 1), (2, 3)):
+            for c in range(2):
+                for t in pair:
+                    update(t, c)
+                    if c == 1:
+                        nc.sync.dma_start(out_rows[t], page[t][:])

@@ -40,25 +40,25 @@ def tile_picked_dwqhaarhpagex_none_p_kernel(
             nc.sync.dma_start(tile[:].bitcast(I32), src[0].rearrange("p n t -> p (n t)").bitcast(I32))
             return tile
 
-        def load_plane(name, src, clear):
+        def load_plane(name, src, clear, queues):
             tile = held.tile([P, src.shape[2]], U8, name=name, tag=name, align_bytes=64)
             clear.memset(tile[:].bitcast(I32), 0)
-            for q in range(4):
-                nc.scalar.dma_start(tile[32 * q : 32 * q + 4, :].bitcast(I32), src[0, 4 * q : 4 * q + 4, :].bitcast(I32))
+            for q, queue in enumerate(queues):
+                queue.dma_start(tile[32 * q : 32 * q + 4, :].bitcast(I32), src[0, 4 * q : 4 * q + 4, :].bitcast(I32))
             return tile
 
-        d_plane = load_plane("d_plane", d_scales, nc.vector)
-        x_plane = load_plane("x_plane", x_scales, nc.gpsimd)
+        d_plane = load_plane("d_plane", d_scales, nc.gpsimd, (nc.scalar, nc.sync, nc.scalar, nc.sync))
+        x_plane = load_plane("x_plane", x_scales, nc.vector, (nc.scalar,) * 4)
         ci_l = load_list("ci_l", ci)
         offs_l = load_list("offs_l", offs)
         d_tab = load_words("d_tab", d_words)
-        x_tab = load_words("x_tab", x_words)
         k1_l = load_list("k1_l", k1)
+        n1_l = load_list("n1_l", n1)
+        x_tab = load_words("x_tab", x_words)
         run_plane = held.tile([P, G], U8, name="run_plane", tag="run_plane", align_bytes=64)
         nc.vector.memset(run_plane[:].bitcast(I32), 0)
         for b in range(2):
             nc.sync.dma_start(run_plane[b:P:16, :].bitcast(I32), d_scales[0, b:16:2, :].bitcast(I32))
-        n1_l = load_list("n1_l", n1)
         n2_l = load_list("n2_l", n2)
         n3_l = load_list("n3_l", n3)
         n4_l = load_list("n4_l", n4)
@@ -75,15 +75,18 @@ def tile_picked_dwqhaarhpagex_none_p_kernel(
         def dealt(tile):
             return tile[:].rearrange("p (t m) -> p m t", t=PACK)
 
-        def in_order(tile):
-            return tile[:].rearrange("p (m t) -> p m t", t=PACK)
+        def deal(dst, src, line):
+            nc.vector.tensor_copy(
+                dst[:].rearrange("p (t c i) -> p c t i", t=PACK, i=line),
+                src[:].rearrange("p (c i t) -> p c t i", t=PACK, i=line),
+            )
 
         ci_scale = held.tile([P, H], U8, name="ci_scale", align_bytes=64)
         nc.vector.tensor_copy(dealt(ci_scale), d_plane[:].indirect(ci_l[:]))
-        x_scale = held.tile([P, S], U8, name="x_scale", align_bytes=64)
-        nc.vector.tensor_copy(x_scale[:], x_plane[:].indirect(offs_l[:]))
         ci_code = held.tile([P, H], U32, name="ci_code", tag="d_plane", align_bytes=64)
         nc.vector.tensor_copy(dealt(ci_code), d_tab[:].indirect(ci_l[:]))
+        x_scale = held.tile([P, S], U8, name="x_scale", align_bytes=64)
+        nc.vector.tensor_copy(x_scale[:], x_plane[:].indirect(offs_l[:]))
         x_code = held.tile([P, S], U32, name="x_code", tag="x_plane", align_bytes=64)
         nc.vector.tensor_copy(x_code[:], x_tab[:].indirect(offs_l[:]))
 
@@ -99,7 +102,7 @@ def tile_picked_dwqhaarhpagex_none_p_kernel(
         k1_bytes = held.tile([P, H], U8, name="k1_bytes", tag="x_tab", align_bytes=64)
         nc.vector.tensor_copy(k1_bytes[:], run_plane[:].indirect(k1_l[:]))
         k1_bytes_dealt = held.tile([P, H], U8, name="k1_bytes_dealt")
-        nc.vector.tensor_copy(dealt(k1_bytes_dealt), in_order(k1_bytes))
+        deal(k1_bytes_dealt, k1_bytes, 16)
         k1_scale = held.tile([P, H], U8, name="k1_scale", align_bytes=64)
         nc.gpsimd.memset(k1_scale[:].bitcast(I32), 0)
         for odd in range(2):
@@ -130,9 +133,11 @@ def tile_picked_dwqhaarhpagex_none_p_kernel(
             pb[t] = held.tile([P, W], F32, name="pb%d" % t, tag="pb%d" % t, align_bytes=64)
             nc.scalar.activation(pb[t][:], neg_pb[t][:], COPY, scale=-1.0)
 
-        def put_pairs(t):
-            dt[t] = held.tile([P, S], F32, name="dt", bufs=2)
+        def put_difference(t):
+            dt[t] = held.tile([P, S], F32, name="dt%d" % t)
             nc.vector.tensor_tensor(dt[t][:].indirect(n2_l[:]), pa[t][:], neg_pb[t][:], ALU.add)
+
+        def put_sum(t):
             nc.vector.tensor_tensor(dt[t][:].indirect(n1_l[:]), pa[t][:], pb[t][:], ALU.add)
 
         def cols_of(c):
@@ -159,40 +164,35 @@ def tile_picked_dwqhaarhpagex_none_p_kernel(
             nc.scalar.activation(half_old[t][:], page[t][:].indirect(n4_l[:]), COPY, scale=0.5)
 
         whole = [slice(0, S)]
-        leave_bank(0)
-        fetch_pairs(0)
-        leave_bank(1)
-        turn_sign(0)
-        fetch_pairs(1)
-        turn_sign(1)
-        put_pairs(0)
-        leave_bank(2)
-        fetch_pairs(2)
-        turn_sign(2)
-        put_pairs(1)
-        fetch_far(0)
-        leave_bank(3)
-        fetch_pairs(3)
-        turn_sign(3)
-        take_top(0, whole)
-        put_pairs(2)
-        fetch_far(1)
-        weigh(0, 0)
-        weigh(0, 1)
-        take_top(1, whole)
+        for t in (0, 1):
+            leave_bank(t)
+            fetch_pairs(t)
+            put_difference(t)
+        for t in (0, 1):
+            turn_sign(t)
+            put_sum(t)
+        for t in (2, 3):
+            leave_bank(t)
+            fetch_pairs(t)
+            put_difference(t)
+        for t in (0, 1):
+            fetch_far(t)
+            take_top(t, whole)
+        for t in (2, 3):
+            turn_sign(t)
+            put_sum(t)
+        for t in (0, 1):
+            weigh(t, 0)
+            weigh(t, 1)
         fetch_old(0, "top0")
-        put_pairs(3)
         fetch_far(2)
-        weigh(1, 0)
-        weigh(1, 1)
-        fetch_old(1, "top1")
-        take_top(2, whole)
         fetch_far(3)
+        take_top(2, whole)
 
         k1_words = held.tile([P, H], U32, name="k1_words", tag="pb3", align_bytes=64)
         nc.vector.tensor_copy(k1_words[:], d_tab[:].indirect(k1_l[:]))
         k1_code = held.tile([P, H], U32, name="k1_code", align_bytes=64)
-        nc.vector.tensor_copy(dealt(k1_code), in_order(k1_words))
+        deal(k1_code, k1_words, 4)
 
         take_top(3, [cols_of(0), cols_of(1)])
         z_code, z_scale = [], []
@@ -211,24 +211,34 @@ def tile_picked_dwqhaarhpagex_none_p_kernel(
             )
             for t in range(PACK):
                 cols = slice(t * P, (t + 1) * P)
-                h_bank[t, c] = psum.tile([P, S], F32, name="bank")
+                if t == 0 or c == 0:
+                    h_bank[t, c] = psum.tile([P, S], F32, name="bank")
+                else:
+                    h_bank[t, c] = h_bank[t, 0]
                 nc.tensor.matmul_mx(
-                    out=h_bank[t, c][:, 0:HALF], lhsT=k1_code[:, cols].bitcast(FP8X4), lhsT_scale=k1_scale[:, cols],
+                    out=h_bank[t, c][:, cols_of(c)], lhsT=k1_code[:, cols].bitcast(FP8X4), lhsT_scale=k1_scale[:, cols],
                     rhs=z_code[c][:].bitcast(FP8X4), rhs_scale=z_scale[c][:], start=True, stop=True,
                 )
+        fetch_old(1, "top1")
         fetch_old(2, "top2")
         fetch_old(3, "top3")
 
-        def update(t, c):
-            new = held.tile([P, HALF], F32, name="new", bufs=2)
+        def take_new(t, c, cols):
+            new = held.tile([P, cols.stop - cols.start], F32, name="new%d_%d" % (t, c))
             nc.vector.scalar_tensor_tensor(
-                new[:], h_bank[t, c][:, 0:HALF], 0.0625, half_old[t][:, cols_of(c)], ALU.mult, ALU.max
+                new[:], h_bank[t, c][:, cols], 0.0625, half_old[t][:, cols], ALU.mult, ALU.max
             )
-            nc.vector.tensor_copy(page[t][:].indirect(entries(n4_l, c)), new[:])
+            return new
 
-        for pair in ((0, 1), (2, 3)):
-            for c in range(2):
-                for t in pair:
-                    update(t, c)
-                    if c == 1:
-                        nc.sync.dma_start(out_rows[t], page[t][:])
+        def put_new(t, cols, new):
+            places = n4_l[:, cols.start // PER_COL : cols.stop // PER_COL]
+            nc.vector.tensor_copy(page[t][:].indirect(places), new[:])
+            if cols.stop == S:
+                nc.sync.dma_start(out_rows[t], page[t][:])
+
+        steps = [(0, 0, cols_of(0)), (0, 1, cols_of(1))] + [(t, 0, whole[0]) for t in range(1, PACK)]
+        ready = take_new(*steps[0])
+        for i, (t, c, cols) in enumerate(steps):
+            ahead = take_new(*steps[i + 1]) if i + 1 < len(steps) else None
+            put_new(t, cols, ready)
+            ready = ahead

@@ -101,27 +101,17 @@ def tile_picked_dwqhaarhpagex_none_p_kernel(
 
         k1_bytes = held.tile([P, H], U8, name="k1_bytes", tag="x_tab", align_bytes=64)
         nc.vector.tensor_copy(k1_bytes[:], run_plane[:].indirect(k1_l[:]))
-        k1_bytes_dealt = held.tile([P, H], U8, name="k1_bytes_dealt")
-        deal(k1_bytes_dealt, k1_bytes, 16)
-        k1_scale = held.tile([P, H], U8, name="k1_scale", align_bytes=64)
-        nc.gpsimd.memset(k1_scale[:].bitcast(I32), 0)
-        for odd in range(2):
-            for b in range(2):
-                nc.sync.dma_start(
-                    k1_scale[2 * odd + b : P : 32, :].bitcast(I32),
-                    k1_bytes_dealt[16 * odd + b : P : 32, :].bitcast(I32),
-                )
 
         pa, pb, neg_pb, dt, far, top, half_old = {}, {}, {}, {}, {}, {}, {}
-        z_pairs = [held.tile([P, 2, HALF, 2], BF16, name="z_pairs%d" % c) for c in range(2)]
+        z_pairs = [held.tile([P, 2, HALF, 2], BF16, name="z_pairs%d" % c, tag="z_pairs%d" % c, align_bytes=64) for c in range(2)]
         s = {}
 
         def leave_bank(t):
-            s[t] = held.tile([P, S], F32, name="s%d" % t)
+            s[t] = held.tile([P, S], F32, name="s%d" % t, tag="s%d" % t, align_bytes=64)
             nc.scalar.activation(s[t][:], s_bank[t][:], COPY, scale=0.0625)
 
         def fetch_pairs(t):
-            pa[t] = held.tile([P, W], F32, name="pa%d" % t)
+            pa[t] = held.tile([P, W], F32, name="pa%d" % t, tag="pa%d" % t, align_bytes=64)
             neg_pb[t] = held.tile([P, W], F32, name="neg_pb%d" % t)
             nc.scalar.activation(pa[t][:], s[t][:].indirect(n1_l[:]), COPY)
             if t == 0:
@@ -147,27 +137,46 @@ def tile_picked_dwqhaarhpagex_none_p_kernel(
             return lst[:, c * HALF // PER_COL : (c + 1) * HALF // PER_COL]
 
         def fetch_far(t):
+            tail = held.tile([P, HALF], F32, name="far_first", tag="far_first", align_bytes=64) if t == 3 else None
             far[t] = held.tile([P, S], F32, name="far%d" % t)
+            far[t, 0] = tail[:] if t == 3 else far[t][:, cols_of(0)]
+            far[t, 1] = far[t][:, cols_of(1)]
             for c in range(2):
-                nc.scalar.activation(far[t][:, cols_of(c)], dt[t][:].indirect(entries(n3_l, c)), COPY)
+                nc.scalar.activation(far[t, c], dt[t][:].indirect(entries(n3_l, c)), COPY)
 
-        def take_top(t, chunks):
-            top[t] = held.tile([P, S], F32, name="top%d" % t, tag="top%d" % t)
+        def take_top(t, chunks, slot):
+            top[t] = held.tile([P, S], F32, name="top%d" % t, tag=slot, align_bytes=64)
             for cols in chunks:
                 nc.vector.tensor_tensor(top[t][:, cols], dt[t][:, cols], far[t][:, cols], ALU.max)
+
+        def take_top_half(t, c):
+            nc.vector.tensor_tensor(top[t][:, cols_of(c)], dt[t][:, cols_of(c)], far[t, c], ALU.max)
 
         def weigh(t, c):
             nc.scalar.activation(z_pairs[c][:, t // 2, :, t % 2], top[t][:, cols_of(c)], COPY, scale=gs_t[:, t : t + 1])
 
         def fetch_old(t, slot):
-            half_old[t] = held.tile([P, S], F32, name="half_old%d" % t, tag=slot)
+            half_old[t] = held.tile([P, S], F32, name="half_old%d" % t, tag=slot, align_bytes=64)
             nc.scalar.activation(half_old[t][:], page[t][:].indirect(n4_l[:]), COPY, scale=0.5)
 
         whole = [slice(0, S)]
-        for t in (0, 1):
-            leave_bank(t)
-            fetch_pairs(t)
-            put_difference(t)
+        leave_bank(0)
+        fetch_pairs(0)
+        k1_bytes_dealt = held.tile([P, H], U8, name="k1_bytes_dealt")
+        deal(k1_bytes_dealt, k1_bytes, 16)
+        k1_scale = held.tile([P, H], U8, name="k1_scale", align_bytes=64)
+        nc.gpsimd.memset(k1_scale[:].bitcast(I32), 0)
+        for odd in range(2):
+            for b in range(2):
+                nc.sync.dma_start(
+                    k1_scale[2 * odd + b : P : 32, :].bitcast(I32),
+                    k1_bytes_dealt[16 * odd + b : P : 32, :].bitcast(I32),
+                )
+
+        put_difference(0)
+        leave_bank(1)
+        fetch_pairs(1)
+        put_difference(1)
         for t in (0, 1):
             turn_sign(t)
             put_sum(t)
@@ -177,57 +186,53 @@ def tile_picked_dwqhaarhpagex_none_p_kernel(
             put_difference(t)
         for t in (0, 1):
             fetch_far(t)
-            take_top(t, whole)
+        take_top(0, whole, "top0")
         for t in (2, 3):
             turn_sign(t)
             put_sum(t)
-        for t in (0, 1):
-            weigh(t, 0)
-            weigh(t, 1)
-        fetch_old(0, "top0")
+        fetch_old(0, "s3")
+        weigh(0, 0)
+        weigh(0, 1)
         fetch_far(2)
         fetch_far(3)
-        take_top(2, whole)
+        take_top(2, whole, "top2")
+        take_top(1, whole, "pa3")
 
-        k1_words = held.tile([P, H], U32, name="k1_words", tag="pb3", align_bytes=64)
+        take_top(3, [], "top3")
+        take_top_half(3, 0)
+        k1_words = held.tile([P, H], U32, name="k1_words", tag="far_first", align_bytes=64)
         nc.vector.tensor_copy(k1_words[:], d_tab[:].indirect(k1_l[:]))
         k1_code = held.tile([P, H], U32, name="k1_code", align_bytes=64)
-        deal(k1_code, k1_words, 4)
+        take_top_half(3, 1)
+        z_code = held.tile([P, S], U32, name="z_code", align_bytes=64)
+        z_scale = held.tile([P, S], U8, name="z_scale", align_bytes=64)
 
-        take_top(3, [cols_of(0), cols_of(1)])
-        z_code, z_scale = [], []
-        h_bank = {}
-        for c in range(2):
-            weigh(2, c)
-            weigh(3, c)
-            z = held.tile([P, HALF, 2], F32, name="z%d" % c, align_bytes=64)
+        def weave(c):
+            for t in range(1, PACK):
+                weigh(t, c)
+            z = held.tile([P, HALF, 2], F32, name="z%d" % c, tag="z%d" % c, align_bytes=64)
             nc.vector.tensor_copy(
                 z[:], z_pairs[c][:].rearrange("p u j e -> p u (j e)").bitcast(F32).rearrange("p u j -> p j u")
             )
-            z_code.append(held.tile([P, HALF], U32, name="z_code%d" % c, align_bytes=64))
-            z_scale.append(held.tile([P, HALF], U8, name="z_scale%d" % c, align_bytes=64))
-            nc.vector.quantize_mx(
-                out=z_code[c][:].bitcast(FP8X4), scales=z_scale[c][:], in_=z[:].rearrange("p j u -> p (j u)").bitcast(BF16)
-            )
-            for t in range(PACK):
-                cols = slice(t * P, (t + 1) * P)
-                if t == 0 or c == 0:
-                    h_bank[t, c] = psum.tile([P, S], F32, name="bank")
-                else:
-                    h_bank[t, c] = h_bank[t, 0]
-                nc.tensor.matmul_mx(
-                    out=h_bank[t, c][:, cols_of(c)], lhsT=k1_code[:, cols].bitcast(FP8X4), lhsT_scale=k1_scale[:, cols],
-                    rhs=z_code[c][:].bitcast(FP8X4), rhs_scale=z_scale[c][:], start=True, stop=True,
-                )
-        fetch_old(1, "top1")
-        fetch_old(2, "top2")
-        fetch_old(3, "top3")
+            return z
 
-        def take_new(t, c, cols):
-            new = held.tile([P, cols.stop - cols.start], F32, name="new%d_%d" % (t, c))
-            nc.vector.scalar_tensor_tensor(
-                new[:], h_bank[t, c][:, cols], 0.0625, half_old[t][:, cols], ALU.mult, ALU.max
+        def quantise(c, z):
+            nc.vector.quantize_mx(
+                out=z_code[:, cols_of(c)].bitcast(FP8X4),
+                scales=z_scale[:, cols_of(c)],
+                in_=z[:].rearrange("p j u -> p (j u)").bitcast(BF16),
             )
+
+        def take_new(t, cols):
+            width = cols.stop - cols.start
+            rows = slice(t * P, (t + 1) * P)
+            bank = psum.tile([P, S], F32, name="bank")
+            nc.tensor.matmul_mx(
+                out=bank[:, 0:width], lhsT=k1_code[:, rows].bitcast(FP8X4), lhsT_scale=k1_scale[:, rows],
+                rhs=z_code[:, cols].bitcast(FP8X4), rhs_scale=z_scale[:, cols], start=True, stop=True,
+            )
+            new = held.tile([P, width], F32, name="new%d_%d" % (t, cols.start))
+            nc.vector.scalar_tensor_tensor(new[:], bank[:, 0:width], 0.0625, half_old[t][:, cols], ALU.mult, ALU.max)
             return new
 
         def put_new(t, cols, new):
@@ -236,9 +241,18 @@ def tile_picked_dwqhaarhpagex_none_p_kernel(
             if cols.stop == S:
                 nc.sync.dma_start(out_rows[t], page[t][:])
 
-        steps = [(0, 0, cols_of(0)), (0, 1, cols_of(1))] + [(t, 0, whole[0]) for t in range(1, PACK)]
+        z_first = weave(0)
+        deal(k1_code, k1_words, 4)
+        quantise(0, z_first)
+        z_second = weave(1)
+        new = take_new(0, cols_of(0))
+        quantise(1, z_second)
+        put_new(0, cols_of(0), new)
+        for t, slot in ((1, "top3"), (2, "z_pairs1"), (3, "z1")):
+            fetch_old(t, slot)
+        steps = [(0, cols_of(1))] + [(t, whole[0]) for t in range(1, PACK)]
         ready = take_new(*steps[0])
-        for i, (t, c, cols) in enumerate(steps):
+        for i, (t, cols) in enumerate(steps):
             ahead = take_new(*steps[i + 1]) if i + 1 < len(steps) else None
             put_new(t, cols, ready)
             ready = ahead

@@ -2,7 +2,7 @@ from contextlib import ExitStack
 
 import concourse.mybir as mybir
 
-K, T, S, G, H, W, U = 512, 2048, 512, 2048, 512, 256, 1024
+K, S, G, H, W, U = 512, 512, 2048, 512, 256, 1024
 FLOPS = 2 * K * H * S + 2 * H * H * S
 
 F32 = mybir.dt.float32
@@ -17,8 +17,14 @@ COPY = mybir.ActivationFunctionType.Copy
 
 P = 128
 PACK = 4
+QUAD = 32
+GROUP = 16
+BLOCKS = K // 32
+LINE = 16
+LAST = PACK - 1
 HALF = S // 2
-PER_COL = 16
+HALVES = (slice(0, HALF), slice(HALF, S))
+WHOLE = slice(0, S)
 
 
 def tile_picked_dwqhaarhpagex_none_p_kernel(
@@ -30,187 +36,188 @@ def tile_picked_dwqhaarhpagex_none_p_kernel(
         held = ctx.enter_context(tc.tile_pool(name="held", bufs=1))
         psum = ctx.enter_context(tc.psum_pool(name="psum", bufs=8))
 
+        def sbuf(name, shape, dtype, after=None):
+            return held.tile(shape, dtype, name=name, tag=after or name, align_bytes=64)
+
+        def entries(offsets, cols):
+            return offsets[:, cols.start // GROUP : cols.stop // GROUP]
+
         def load_list(name, src):
-            tile = lists.tile([P, src.shape[1]], U16, name=name)
-            nc.sync.dma_start(tile[:], src)
-            return tile
+            offsets = lists.tile([P, src.shape[1]], U16, name=name)
+            nc.sync.dma_start(offsets[:], src)
+            return offsets
 
         def load_words(name, src):
-            tile = held.tile([P, src.shape[2]], U32, name=name, tag=name, align_bytes=64)
-            nc.sync.dma_start(tile[:].bitcast(I32), src[0].rearrange("p n t -> p (n t)").bitcast(I32))
-            return tile
+            table = sbuf(name, [P, src.shape[2]], U32)
+            nc.sync.dma_start(table[:].bitcast(I32), src[0].rearrange("p n t -> p (n t)").bitcast(I32))
+            return table
 
-        def load_plane(name, src, clear, queues):
-            tile = held.tile([P, src.shape[2]], U8, name=name, tag=name, align_bytes=64)
-            clear.memset(tile[:].bitcast(I32), 0)
+        def cleared_plane(name, columns, engine):
+            plane = sbuf(name, [P, columns], U8)
+            engine.memset(plane[:].bitcast(I32), 0)
+            return plane
+
+        def load_plane(name, src, engine, queues):
+            plane = cleared_plane(name, src.shape[2], engine)
             for q, queue in enumerate(queues):
-                queue.dma_start(tile[32 * q : 32 * q + 4, :].bitcast(I32), src[0, 4 * q : 4 * q + 4, :].bitcast(I32))
-            return tile
+                queue.dma_start(
+                    plane[QUAD * q : QUAD * q + PACK, :].bitcast(I32), src[0, PACK * q : PACK * (q + 1), :].bitcast(I32)
+                )
+            return plane
 
         d_plane = load_plane("d_plane", d_scales, nc.gpsimd, (nc.scalar, nc.sync, nc.scalar, nc.sync))
-        x_plane = load_plane("x_plane", x_scales, nc.vector, (nc.scalar,) * 4)
+        x_plane = load_plane("x_plane", x_scales, nc.vector, (nc.scalar,) * PACK)
         ci_l = load_list("ci_l", ci)
         offs_l = load_list("offs_l", offs)
-        d_tab = load_words("d_tab", d_words)
+        d_table = load_words("d_table", d_words)
         k1_l = load_list("k1_l", k1)
         n1_l = load_list("n1_l", n1)
-        x_tab = load_words("x_tab", x_words)
-        run_plane = held.tile([P, G], U8, name="run_plane", tag="run_plane", align_bytes=64)
-        nc.vector.memset(run_plane[:].bitcast(I32), 0)
+        x_table = load_words("x_table", x_words)
+        run_bytes = cleared_plane("run_bytes", G, nc.vector)
         for b in range(2):
-            nc.sync.dma_start(run_plane[b:P:16, :].bitcast(I32), d_scales[0, b:16:2, :].bitcast(I32))
+            nc.sync.dma_start(run_bytes[b:P:GROUP, :].bitcast(I32), d_scales[0, b:BLOCKS:2, :].bitcast(I32))
         n2_l = load_list("n2_l", n2)
         n3_l = load_list("n3_l", n3)
         n4_l = load_list("n4_l", n4)
-        gs_t = held.tile([P, PACK], F32, name="gs_t")
+        gs_t = sbuf("gs_t", [P, PACK], F32)
         nc.sync.dma_start(gs_t[:], gs.rearrange("(p t) o -> p (t o)", t=PACK))
         mem_rows = mem.rearrange("(p t) u -> t p u", t=PACK)
         out_rows = out.rearrange("(p t) u -> t p u", t=PACK)
-
         page = []
         for t in range(PACK):
-            page.append(held.tile([P, U], F32, name="page%d" % t))
+            page.append(sbuf("page%d" % t, [P, U], F32))
             nc.sync.dma_start(page[t][:], mem_rows[t])
 
         def dealt(tile):
             return tile[:].rearrange("p (t m) -> p m t", t=PACK)
 
-        def deal(dst, src, line):
+        def deal(dst, src, run):
             nc.vector.tensor_copy(
-                dst[:].rearrange("p (t c i) -> p c t i", t=PACK, i=line),
-                src[:].rearrange("p (c i t) -> p c t i", t=PACK, i=line),
+                dst[:].rearrange("p (t c i) -> p c t i", t=PACK, i=run),
+                src[:].rearrange("p (c i t) -> p c t i", t=PACK, i=run),
             )
 
-        ci_scale = held.tile([P, H], U8, name="ci_scale", align_bytes=64)
+        ci_scale = sbuf("ci_scale", [P, H], U8)
         nc.vector.tensor_copy(dealt(ci_scale), d_plane[:].indirect(ci_l[:]))
-        ci_code = held.tile([P, H], U32, name="ci_code", tag="d_plane", align_bytes=64)
-        nc.vector.tensor_copy(dealt(ci_code), d_tab[:].indirect(ci_l[:]))
-        x_scale = held.tile([P, S], U8, name="x_scale", align_bytes=64)
+        ci_code = sbuf("ci_code", [P, H], U32, after="d_plane")
+        nc.vector.tensor_copy(dealt(ci_code), d_table[:].indirect(ci_l[:]))
+        x_scale = sbuf("x_scale", [P, S], U8)
         nc.vector.tensor_copy(x_scale[:], x_plane[:].indirect(offs_l[:]))
-        x_code = held.tile([P, S], U32, name="x_code", tag="x_plane", align_bytes=64)
-        nc.vector.tensor_copy(x_code[:], x_tab[:].indirect(offs_l[:]))
+        x_code = sbuf("x_code", [P, S], U32, after="x_plane")
+        nc.vector.tensor_copy(x_code[:], x_table[:].indirect(offs_l[:]))
 
-        s_bank = []
-        for t in range(PACK):
-            cols = slice(t * P, (t + 1) * P)
-            s_bank.append(psum.tile([P, S], F32, name="bank"))
+        def product(t, left_code, left_scale, right_code, right_scale):
+            rows = slice(t * P, (t + 1) * P)
+            bank = psum.tile([P, S], F32, name="bank")
+            sums = bank[:, 0 : right_code.shape[1]]
             nc.tensor.matmul_mx(
-                out=s_bank[t][:], lhsT=ci_code[:, cols].bitcast(FP8X4), lhsT_scale=ci_scale[:, cols],
-                rhs=x_code[:].bitcast(FP8X4), rhs_scale=x_scale[:], start=True, stop=True,
+                out=sums,
+                lhsT=left_code[:, rows].bitcast(FP8X4),
+                lhsT_scale=left_scale[:, rows],
+                rhs=right_code.bitcast(FP8X4),
+                rhs_scale=right_scale,
+                start=True,
+                stop=True,
             )
+            return sums
 
-        k1_bytes = held.tile([P, H], U8, name="k1_bytes", tag="x_tab", align_bytes=64)
-        nc.vector.tensor_copy(k1_bytes[:], run_plane[:].indirect(k1_l[:]))
+        s_sums = [product(t, ci_code, ci_scale, x_code[:], x_scale[:]) for t in range(PACK)]
 
-        pa, pb, neg_pb, dt, far, top, half_old = {}, {}, {}, {}, {}, {}, {}
-        z_pairs = [held.tile([P, 2, HALF, 2], BF16, name="z_pairs%d" % c, tag="z_pairs%d" % c, align_bytes=64) for c in range(2)]
-        s = {}
+        k1_bytes = sbuf("k1_bytes", [P, H], U8, after="x_table")
+        nc.vector.tensor_copy(k1_bytes[:], run_bytes[:].indirect(k1_l[:]))
 
-        def leave_bank(t):
-            s[t] = held.tile([P, S], F32, name="s%d" % t, tag="s%d" % t, align_bytes=64)
-            nc.scalar.activation(s[t][:], s_bank[t][:], COPY, scale=0.0625)
+        s, pa, pb, neg_pb, dt, far, top, half_old = {}, {}, {}, {}, {}, {}, {}, {}
+        z_pairs = [sbuf("z_pairs%d" % c, [P, 2, HALF, 2], BF16) for c in range(2)]
 
         def fetch_pairs(t):
-            pa[t] = held.tile([P, W], F32, name="pa%d" % t, tag="pa%d" % t, align_bytes=64)
-            neg_pb[t] = held.tile([P, W], F32, name="neg_pb%d" % t)
+            s[t] = sbuf("s%d" % t, [P, S], F32)
+            nc.scalar.activation(s[t][:], s_sums[t], COPY, scale=0.0625)
+            pa[t] = sbuf("pa%d" % t, [P, W], F32)
+            neg_pb[t] = sbuf("neg_pb%d" % t, [P, W], F32)
             nc.scalar.activation(pa[t][:], s[t][:].indirect(n1_l[:]), COPY)
             if t == 0:
                 nc.vector.tensor_scalar(neg_pb[t][:], s[t][:].indirect(n2_l[:]), -1.0, 0.0, ALU.mult, ALU.add)
             else:
                 nc.scalar.activation(neg_pb[t][:], s[t][:].indirect(n2_l[:]), COPY, scale=-1.0)
 
-        def turn_sign(t):
-            pb[t] = held.tile([P, W], F32, name="pb%d" % t, tag="pb%d" % t, align_bytes=64)
-            nc.scalar.activation(pb[t][:], neg_pb[t][:], COPY, scale=-1.0)
-
         def put_difference(t):
-            dt[t] = held.tile([P, S], F32, name="dt%d" % t)
+            dt[t] = sbuf("dt%d" % t, [P, S], F32)
             nc.vector.tensor_tensor(dt[t][:].indirect(n2_l[:]), pa[t][:], neg_pb[t][:], ALU.add)
 
         def put_sum(t):
+            pb[t] = sbuf("pb%d" % t, [P, W], F32)
+            nc.scalar.activation(pb[t][:], neg_pb[t][:], COPY, scale=-1.0)
             nc.vector.tensor_tensor(dt[t][:].indirect(n1_l[:]), pa[t][:], pb[t][:], ALU.add)
 
-        def cols_of(c):
-            return slice(c * HALF, (c + 1) * HALF)
+        def fetch_far(t, dst, cols):
+            nc.scalar.activation(dst, dt[t][:].indirect(entries(n3_l, cols)), COPY)
 
-        def entries(lst, c):
-            return lst[:, c * HALF // PER_COL : (c + 1) * HALF // PER_COL]
+        def fetch_far_row(t):
+            far[t] = sbuf("far%d" % t, [P, S], F32)
+            for cols in HALVES:
+                fetch_far(t, far[t][:, cols], cols)
 
-        def fetch_far(t):
-            tail = held.tile([P, HALF], F32, name="far_first", tag="far_first", align_bytes=64) if t == 3 else None
-            far[t] = held.tile([P, S], F32, name="far%d" % t)
-            far[t, 0] = tail[:] if t == 3 else far[t][:, cols_of(0)]
-            far[t, 1] = far[t][:, cols_of(1)]
-            for c in range(2):
-                nc.scalar.activation(far[t, c], dt[t][:].indirect(entries(n3_l, c)), COPY)
-
-        def take_top(t, chunks, slot):
-            top[t] = held.tile([P, S], F32, name="top%d" % t, tag=slot, align_bytes=64)
-            for cols in chunks:
-                nc.vector.tensor_tensor(top[t][:, cols], dt[t][:, cols], far[t][:, cols], ALU.max)
-
-        def take_top_half(t, c):
-            nc.vector.tensor_tensor(top[t][:, cols_of(c)], dt[t][:, cols_of(c)], far[t, c], ALU.max)
+        def take_top_row(t, after=None):
+            top[t] = sbuf("top%d" % t, [P, S], F32, after)
+            nc.vector.tensor_tensor(top[t][:], dt[t][:], far[t][:], ALU.max)
 
         def weigh(t, c):
-            nc.scalar.activation(z_pairs[c][:, t // 2, :, t % 2], top[t][:, cols_of(c)], COPY, scale=gs_t[:, t : t + 1])
+            nc.scalar.activation(z_pairs[c][:, t // 2, :, t % 2], top[t][:, HALVES[c]], COPY, scale=gs_t[:, t : t + 1])
 
-        def fetch_old(t, slot):
-            half_old[t] = held.tile([P, S], F32, name="half_old%d" % t, tag=slot, align_bytes=64)
+        def fetch_old(t, after):
+            half_old[t] = sbuf("half_old%d" % t, [P, S], F32, after)
             nc.scalar.activation(half_old[t][:], page[t][:].indirect(n4_l[:]), COPY, scale=0.5)
 
-        whole = [slice(0, S)]
-        leave_bank(0)
         fetch_pairs(0)
-        k1_bytes_dealt = held.tile([P, H], U8, name="k1_bytes_dealt")
-        deal(k1_bytes_dealt, k1_bytes, 16)
-        k1_scale = held.tile([P, H], U8, name="k1_scale", align_bytes=64)
-        nc.gpsimd.memset(k1_scale[:].bitcast(I32), 0)
+        k1_bytes_dealt = sbuf("k1_bytes_dealt", [P, H], U8)
+        deal(k1_bytes_dealt, k1_bytes, LINE)
+        k1_scale = cleared_plane("k1_scale", H, nc.gpsimd)
         for odd in range(2):
             for b in range(2):
                 nc.sync.dma_start(
-                    k1_scale[2 * odd + b : P : 32, :].bitcast(I32),
-                    k1_bytes_dealt[16 * odd + b : P : 32, :].bitcast(I32),
+                    k1_scale[2 * odd + b : P : QUAD, :].bitcast(I32),
+                    k1_bytes_dealt[GROUP * odd + b : P : QUAD, :].bitcast(I32),
                 )
-
         put_difference(0)
-        leave_bank(1)
         fetch_pairs(1)
         put_difference(1)
         for t in (0, 1):
-            turn_sign(t)
             put_sum(t)
         for t in (2, 3):
-            leave_bank(t)
             fetch_pairs(t)
             put_difference(t)
         for t in (0, 1):
-            fetch_far(t)
-        take_top(0, whole, "top0")
+            fetch_far_row(t)
+        take_top_row(0)
         for t in (2, 3):
-            turn_sign(t)
             put_sum(t)
-        fetch_old(0, "s3")
-        weigh(0, 0)
-        weigh(0, 1)
-        fetch_far(2)
-        fetch_far(3)
-        take_top(2, whole, "top2")
-        take_top(1, whole, "pa3")
+        fetch_old(0, after="s3")
+        for c in range(2):
+            weigh(0, c)
+        fetch_far_row(2)
 
-        take_top(3, [], "top3")
-        take_top_half(3, 0)
-        k1_words = held.tile([P, H], U32, name="k1_words", tag="far_first", align_bytes=64)
-        nc.vector.tensor_copy(k1_words[:], d_tab[:].indirect(k1_l[:]))
-        k1_code = held.tile([P, H], U32, name="k1_code", align_bytes=64)
-        take_top_half(3, 1)
-        z_code = held.tile([P, S], U32, name="z_code", align_bytes=64)
-        z_scale = held.tile([P, S], U8, name="z_scale", align_bytes=64)
+        far_last = [sbuf("far_last%d" % c, [P, HALF], F32) for c in range(2)]
+        for c in range(2):
+            fetch_far(LAST, far_last[c][:], HALVES[c])
+        take_top_row(2)
+        take_top_row(1, after="pa3")
+        top[LAST] = sbuf("top3", [P, S], F32)
+
+        def take_top_last(c):
+            nc.vector.tensor_tensor(top[LAST][:, HALVES[c]], dt[LAST][:, HALVES[c]], far_last[c][:], ALU.max)
+
+        take_top_last(0)
+        k1_words = sbuf("k1_words", [P, H], U32, after="far_last0")
+        nc.vector.tensor_copy(k1_words[:], d_table[:].indirect(k1_l[:]))
+        k1_code = sbuf("k1_code", [P, H], U32)
+        take_top_last(1)
+        z_code = sbuf("z_code", [P, S], U32)
+        z_scale = sbuf("z_scale", [P, S], U8)
 
         def weave(c):
             for t in range(1, PACK):
                 weigh(t, c)
-            z = held.tile([P, HALF, 2], F32, name="z%d" % c, tag="z%d" % c, align_bytes=64)
+            z = sbuf("z%d" % c, [P, HALF, 2], F32)
             nc.vector.tensor_copy(
                 z[:], z_pairs[c][:].rearrange("p u j e -> p u (j e)").bitcast(F32).rearrange("p u j -> p j u")
             )
@@ -218,39 +225,32 @@ def tile_picked_dwqhaarhpagex_none_p_kernel(
 
         def quantise(c, z):
             nc.vector.quantize_mx(
-                out=z_code[:, cols_of(c)].bitcast(FP8X4),
-                scales=z_scale[:, cols_of(c)],
+                out=z_code[:, HALVES[c]].bitcast(FP8X4),
+                scales=z_scale[:, HALVES[c]],
                 in_=z[:].rearrange("p j u -> p (j u)").bitcast(BF16),
             )
 
         def take_new(t, cols):
-            width = cols.stop - cols.start
-            rows = slice(t * P, (t + 1) * P)
-            bank = psum.tile([P, S], F32, name="bank")
-            nc.tensor.matmul_mx(
-                out=bank[:, 0:width], lhsT=k1_code[:, rows].bitcast(FP8X4), lhsT_scale=k1_scale[:, rows],
-                rhs=z_code[:, cols].bitcast(FP8X4), rhs_scale=z_scale[:, cols], start=True, stop=True,
-            )
-            new = held.tile([P, width], F32, name="new%d_%d" % (t, cols.start))
-            nc.vector.scalar_tensor_tensor(new[:], bank[:, 0:width], 0.0625, half_old[t][:, cols], ALU.mult, ALU.max)
+            sums = product(t, k1_code, k1_scale, z_code[:, cols], z_scale[:, cols])
+            new = sbuf("new%d_%d" % (t, cols.start), [P, cols.stop - cols.start], F32)
+            nc.vector.scalar_tensor_tensor(new[:], sums, 0.0625, half_old[t][:, cols], ALU.mult, ALU.max)
             return new
 
         def put_new(t, cols, new):
-            places = n4_l[:, cols.start // PER_COL : cols.stop // PER_COL]
-            nc.vector.tensor_copy(page[t][:].indirect(places), new[:])
+            nc.vector.tensor_copy(page[t][:].indirect(entries(n4_l, cols)), new[:])
             if cols.stop == S:
                 nc.sync.dma_start(out_rows[t], page[t][:])
 
         z_first = weave(0)
-        deal(k1_code, k1_words, 4)
+        deal(k1_code, k1_words, LINE // 4)
         quantise(0, z_first)
         z_second = weave(1)
-        new = take_new(0, cols_of(0))
+        new_first = take_new(0, HALVES[0])
         quantise(1, z_second)
-        put_new(0, cols_of(0), new)
-        for t, slot in ((1, "top3"), (2, "z_pairs1"), (3, "z1")):
-            fetch_old(t, slot)
-        steps = [(0, cols_of(1))] + [(t, whole[0]) for t in range(1, PACK)]
+        put_new(0, HALVES[0], new_first)
+        for t, after in ((1, "top3"), (2, "z_pairs1"), (3, "z1")):
+            fetch_old(t, after)
+        steps = [(0, HALVES[1])] + [(t, WHOLE) for t in range(1, PACK)]
         ready = take_new(*steps[0])
         for i, (t, cols) in enumerate(steps):
             ahead = take_new(*steps[i + 1]) if i + 1 < len(steps) else None

from contextlib import ExitStack

import concourse.mybir as mybir

K, S, G, H, W, U = 512, 512, 2048, 512, 256, 1024
FLOPS = 2 * K * H * S + 2 * H * H * S

F32 = mybir.dt.float32
BF16 = mybir.dt.bfloat16
I32 = mybir.dt.int32
U32 = mybir.dt.uint32
U16 = mybir.dt.uint16
U8 = mybir.dt.uint8
FP8X4 = mybir.dt.float8_e4m3fn_x4
ALU = mybir.AluOpType
COPY = mybir.ActivationFunctionType.Copy

P = 128
PACK = 4
QUAD = 32
GROUP = 16
BLOCKS = K // 32
LINE = 16
LAST = PACK - 1
HALF = S // 2
HALVES = (slice(0, HALF), slice(HALF, S))
WHOLE = slice(0, S)


def tile_picked_dwqhaarhpagex_none_p_kernel(
    tc, x_words, x_scales, d_words, d_scales, gs, mem, offs, ci, n1, n2, n3, k1, n4, out
):
    nc = tc.nc
    with ExitStack() as ctx:
        lists = ctx.enter_context(tc.tile_pool(name="lists", bufs=1))
        held = ctx.enter_context(tc.tile_pool(name="held", bufs=1))
        psum = ctx.enter_context(tc.psum_pool(name="psum", bufs=8))

        def sbuf(name, shape, dtype, after=None):
            return held.tile(shape, dtype, name=name, tag=after or name, align_bytes=64)

        def entries(offsets, cols):
            return offsets[:, cols.start // GROUP : cols.stop // GROUP]

        def load_list(name, src):
            offsets = lists.tile([P, src.shape[1]], U16, name=name)
            nc.sync.dma_start(offsets[:], src)
            return offsets

        def load_words(name, src):
            table = sbuf(name, [P, src.shape[2]], U32)
            nc.sync.dma_start(table[:].bitcast(I32), src[0].rearrange("p n t -> p (n t)").bitcast(I32))
            return table

        def cleared_plane(name, columns, engine):
            plane = sbuf(name, [P, columns], U8)
            engine.memset(plane[:].bitcast(I32), 0)
            return plane

        def load_plane(name, src, engine, queues):
            plane = cleared_plane(name, src.shape[2], engine)
            for q, queue in enumerate(queues):
                queue.dma_start(
                    plane[QUAD * q : QUAD * q + PACK, :].bitcast(I32), src[0, PACK * q : PACK * (q + 1), :].bitcast(I32)
                )
            return plane

        d_plane = load_plane("d_plane", d_scales, nc.gpsimd, (nc.scalar, nc.sync, nc.scalar, nc.sync))
        x_plane = load_plane("x_plane", x_scales, nc.vector, (nc.scalar,) * PACK)
        ci_l = load_list("ci_l", ci)
        offs_l = load_list("offs_l", offs)
        d_table = load_words("d_table", d_words)
        k1_l = load_list("k1_l", k1)
        n1_l = load_list("n1_l", n1)
        x_table = load_words("x_table", x_words)
        run_bytes = cleared_plane("run_bytes", G, nc.vector)
        for b in range(2):
            nc.sync.dma_start(run_bytes[b:P:GROUP, :].bitcast(I32), d_scales[0, b:BLOCKS:2, :].bitcast(I32))
        n2_l = load_list("n2_l", n2)
        n3_l = load_list("n3_l", n3)
        n4_l = load_list("n4_l", n4)
        gs_t = sbuf("gs_t", [P, PACK], F32)
        nc.sync.dma_start(gs_t[:], gs.rearrange("(p t) o -> p (t o)", t=PACK))
        mem_rows = mem.rearrange("(p t) u -> t p u", t=PACK)
        out_rows = out.rearrange("(p t) u -> t p u", t=PACK)
        page = []
        for t in range(PACK):
            page.append(sbuf("page%d" % t, [P, U], F32))
            nc.sync.dma_start(page[t][:], mem_rows[t])

        def dealt(tile):
            return tile[:].rearrange("p (t m) -> p m t", t=PACK)

        def deal(dst, src, run):
            nc.vector.tensor_copy(
                dst[:].rearrange("p (t c i) -> p c t i", t=PACK, i=run),
                src[:].rearrange("p (c i t) -> p c t i", t=PACK, i=run),
            )

        ci_scale = sbuf("ci_scale", [P, H], U8)
        nc.vector.tensor_copy(dealt(ci_scale), d_plane[:].indirect(ci_l[:]))
        ci_code = sbuf("ci_code", [P, H], U32, after="d_plane")
        nc.vector.tensor_copy(dealt(ci_code), d_table[:].indirect(ci_l[:]))
        x_scale = sbuf("x_scale", [P, S], U8)
        nc.vector.tensor_copy(x_scale[:], x_plane[:].indirect(offs_l[:]))
        x_code = sbuf("x_code", [P, S], U32, after="x_plane")
        nc.vector.tensor_copy(x_code[:], x_table[:].indirect(offs_l[:]))

        def product(t, left_code, left_scale, right_code, right_scale):
            rows = slice(t * P, (t + 1) * P)
            bank = psum.tile([P, S], F32, name="bank")
            sums = bank[:, 0 : right_code.shape[1]]
            nc.tensor.matmul_mx(
                out=sums,
                lhsT=left_code[:, rows].bitcast(FP8X4),
                lhsT_scale=left_scale[:, rows],
                rhs=right_code.bitcast(FP8X4),
                rhs_scale=right_scale,
                start=True,
                stop=True,
            )
            return sums

        s_sums = [product(t, ci_code, ci_scale, x_code[:], x_scale[:]) for t in range(PACK)]

        k1_bytes = sbuf("k1_bytes", [P, H], U8, after="x_table")
        nc.vector.tensor_copy(k1_bytes[:], run_bytes[:].indirect(k1_l[:]))

        s, pa, pb, neg_pb, dt, far, top, half_old = {}, {}, {}, {}, {}, {}, {}, {}
        z_pairs = [sbuf("z_pairs%d" % c, [P, 2, HALF, 2], BF16) for c in range(2)]

        def fetch_pairs(t):
            s[t] = sbuf("s%d" % t, [P, S], F32)
            nc.scalar.activation(s[t][:], s_sums[t], COPY, scale=0.0625)
            pa[t] = sbuf("pa%d" % t, [P, W], F32)
            neg_pb[t] = sbuf("neg_pb%d" % t, [P, W], F32)
            nc.scalar.activation(pa[t][:], s[t][:].indirect(n1_l[:]), COPY)
            if t == 0:
                nc.vector.tensor_scalar(neg_pb[t][:], s[t][:].indirect(n2_l[:]), -1.0, 0.0, ALU.mult, ALU.add)
            else:
                nc.scalar.activation(neg_pb[t][:], s[t][:].indirect(n2_l[:]), COPY, scale=-1.0)

        def put_difference(t):
            dt[t] = sbuf("dt%d" % t, [P, S], F32)
            nc.vector.tensor_tensor(dt[t][:].indirect(n2_l[:]), pa[t][:], neg_pb[t][:], ALU.add)

        def put_sum(t):
            pb[t] = sbuf("pb%d" % t, [P, W], F32)
            nc.scalar.activation(pb[t][:], neg_pb[t][:], COPY, scale=-1.0)
            nc.vector.tensor_tensor(dt[t][:].indirect(n1_l[:]), pa[t][:], pb[t][:], ALU.add)

        def fetch_far(t, dst, cols):
            nc.scalar.activation(dst, dt[t][:].indirect(entries(n3_l, cols)), COPY)

        def fetch_far_row(t):
            far[t] = sbuf("far%d" % t, [P, S], F32)
            for cols in HALVES:
                fetch_far(t, far[t][:, cols], cols)

        def take_top_row(t, after=None):
            top[t] = sbuf("top%d" % t, [P, S], F32, after)
            nc.vector.tensor_tensor(top[t][:], dt[t][:], far[t][:], ALU.max)

        def weigh(t, c):
            nc.scalar.activation(z_pairs[c][:, t // 2, :, t % 2], top[t][:, HALVES[c]], COPY, scale=gs_t[:, t : t + 1])

        def fetch_old(t, after):
            half_old[t] = sbuf("half_old%d" % t, [P, S], F32, after)
            nc.scalar.activation(half_old[t][:], page[t][:].indirect(n4_l[:]), COPY, scale=0.5)

        fetch_pairs(0)
        k1_bytes_dealt = sbuf("k1_bytes_dealt", [P, H], U8)
        deal(k1_bytes_dealt, k1_bytes, LINE)
        k1_scale = cleared_plane("k1_scale", H, nc.gpsimd)
        for odd in range(2):
            for b in range(2):
                nc.sync.dma_start(
                    k1_scale[2 * odd + b : P : QUAD, :].bitcast(I32),
                    k1_bytes_dealt[GROUP * odd + b : P : QUAD, :].bitcast(I32),
                )
        put_difference(0)
        fetch_pairs(1)
        put_difference(1)
        for t in (0, 1):
            put_sum(t)
        for t in (2, 3):
            fetch_pairs(t)
            put_difference(t)
        for t in (0, 1):
            fetch_far_row(t)
        take_top_row(0)
        for t in (2, 3):
            put_sum(t)
        fetch_old(0, after="s3")
        for c in range(2):
            weigh(0, c)
        fetch_far_row(2)

        far_last = [sbuf("far_last%d" % c, [P, HALF], F32) for c in range(2)]
        for c in range(2):
            fetch_far(LAST, far_last[c][:], HALVES[c])
        take_top_row(2)
        take_top_row(1, after="pa3")
        top[LAST] = sbuf("top3", [P, S], F32)

        def take_top_last(c):
            nc.vector.tensor_tensor(top[LAST][:, HALVES[c]], dt[LAST][:, HALVES[c]], far_last[c][:], ALU.max)

        take_top_last(0)
        k1_words = sbuf("k1_words", [P, H], U32, after="far_last0")
        nc.vector.tensor_copy(k1_words[:], d_table[:].indirect(k1_l[:]))
        k1_code = sbuf("k1_code", [P, H], U32)
        take_top_last(1)
        z_code = sbuf("z_code", [P, S], U32)
        z_scale = sbuf("z_scale", [P, S], U8)

        def weave(c):
            for t in range(1, PACK):
                weigh(t, c)
            z = sbuf("z%d" % c, [P, HALF, 2], F32)
            nc.vector.tensor_copy(
                z[:], z_pairs[c][:].rearrange("p u j e -> p u (j e)").bitcast(F32).rearrange("p u j -> p j u")
            )
            return z

        def quantise(c, z):
            nc.vector.quantize_mx(
                out=z_code[:, HALVES[c]].bitcast(FP8X4),
                scales=z_scale[:, HALVES[c]],
                in_=z[:].rearrange("p j u -> p (j u)").bitcast(BF16),
            )

        def take_new(t, cols):
            sums = product(t, k1_code, k1_scale, z_code[:, cols], z_scale[:, cols])
            new = sbuf("new%d_%d" % (t, cols.start), [P, cols.stop - cols.start], F32)
            nc.vector.scalar_tensor_tensor(new[:], sums, 0.0625, half_old[t][:, cols], ALU.mult, ALU.max)
            return new

        def put_new(t, cols, new):
            nc.vector.tensor_copy(page[t][:].indirect(entries(n4_l, cols)), new[:])
            if cols.stop == S:
                nc.sync.dma_start(out_rows[t], page[t][:])

        z_first = weave(0)
        deal(k1_code, k1_words, LINE // 4)
        quantise(0, z_first)
        z_second = weave(1)
        new_first = take_new(0, HALVES[0])
        quantise(1, z_second)
        put_new(0, HALVES[0], new_first)
        for t, after in ((1, "top3"), (2, "z_pairs1"), (3, "z1")):
            fetch_old(t, after)
        steps = [(0, HALVES[1])] + [(t, WHOLE) for t in range(1, PACK)]
        ready = take_new(*steps[0])
        for i, (t, cols) in enumerate(steps):
            ahead = take_new(*steps[i + 1]) if i + 1 < len(steps) else None
            put_new(t, cols, ready)
            ready = ahead
